import numpy as np, ml_dtypes
CORES = [12,28,44,60,3,19,35,51]
N = 8
TOK, K = 64, 2
ROUTE = [[[0,2],[2,7],[2,3],[4,7],[3,5],[2,3],[1,3],[4,7],[0,5],[0,3],[2,6],[3,5],[3,5],[2,6],[3,5],[1,6],[2,7],[1,2],[1,2],[3,4],[2,6],[4,7],[2,6],[6,7],[0,7],[2,4],[6,7],[0,3],[0,5],[1,3],[1,5],[2,4],[0,1],[1,2],[0,7],[5,6],[1,3],[0,5],[3,6],[3,4],[3,7],[1,4],[5,6],[3,5],[0,3],[3,7],[2,6],[1,4],[3,4],[1,3],[2,5],[6,7],[0,1],[5,6],[1,2],[1,6],[4,7],[6,7],[2,4],[2,3],[2,4],[4,6],[2,3],[1,2]],[[1,3],[0,2],[2,6],[0,7],[5,6],[1,5],[4,6],[5,7],[1,5],[0,7],[0,2],[5,6],[5,6],[1,7],[4,6],[1,5],[3,6],[3,4],[1,3],[0,3],[0,1],[4,6],[2,5],[2,3],[3,6],[3,7],[0,5],[0,3],[3,5],[2,7],[1,4],[1,5],[2,3],[3,6],[4,7],[1,7],[3,4],[1,7],[0,4],[1,2],[1,2],[0,7],[0,6],[0,3],[1,7],[2,7],[5,6],[0,5],[1,2],[0,4],[5,6],[0,4],[0,4],[4,6],[0,3],[0,3],[4,5],[0,1],[1,3],[1,4],[2,7],[4,5],[0,2],[0,1]],[[1,2],[1,6],[0,4],[4,7],[3,5],[1,7],[0,7],[0,2],[1,3],[0,4],[3,5],[0,1],[1,6],[5,7],[3,7],[6,7],[0,3],[0,6],[1,5],[4,7],[0,1],[1,7],[4,6],[2,6],[0,2],[1,2],[4,7],[5,7],[5,6],[0,3],[3,5],[2,4],[0,6],[5,6],[3,4],[0,3],[0,7],[5,6],[2,4],[0,4],[2,6],[2,7],[6,7],[2,4],[4,6],[0,2],[1,6],[0,4],[1,3],[1,5],[0,2],[5,7],[0,6],[5,6],[0,4],[2,6],[4,6],[0,7],[3,5],[3,4],[5,7],[0,1],[6,7],[2,7]],[[3,4],[1,3],[2,3],[4,7],[0,2],[5,7],[2,5],[4,7],[0,1],[0,4],[1,5],[3,7],[2,4],[4,6],[1,3],[2,4],[0,7],[2,4],[2,6],[2,4],[0,2],[5,7],[5,6],[2,7],[4,6],[1,5],[0,3],[1,7],[1,5],[0,5],[5,7],[4,6],[1,5],[1,5],[1,3],[6,7],[1,2],[1,5],[4,7],[1,2],[4,6],[2,7],[2,6],[0,3],[2,4],[1,2],[0,4],[2,5],[3,6],[4,6],[6,7],[2,6],[4,6],[0,6],[2,3],[0,4],[1,5],[1,4],[0,4],[1,3],[6,7],[5,6],[0,7],[3,6]],[[1,7],[3,4],[1,2],[0,3],[5,7],[5,7],[2,6],[4,7],[0,1],[2,4],[5,7],[6,7],[3,7],[4,5],[4,6],[3,6],[5,7],[4,5],[3,5],[3,4],[5,6],[5,6],[1,3],[1,7],[0,5],[1,6],[2,5],[1,5],[1,2],[5,6],[0,1],[1,6],[5,7],[4,6],[0,3],[5,7],[0,2],[0,7],[2,6],[1,3],[1,2],[1,4],[2,6],[1,5],[0,3],[0,7],[2,5],[2,6],[3,5],[1,2],[0,7],[1,7],[0,6],[5,7],[3,5],[2,7],[1,5],[0,5],[3,5],[1,6],[0,1],[2,3],[1,4],[1,2]],[[1,4],[6,7],[0,2],[1,4],[4,6],[3,6],[4,7],[1,4],[5,6],[2,6],[3,5],[4,5],[1,3],[6,7],[2,5],[4,6],[1,2],[4,6],[1,5],[0,4],[3,6],[4,7],[0,1],[1,7],[1,6],[4,6],[2,5],[1,2],[0,2],[5,6],[3,4],[3,4],[4,6],[4,6],[4,7],[4,7],[2,7],[0,4],[1,2],[4,5],[4,6],[1,5],[1,6],[3,4],[4,5],[5,6],[2,6],[0,2],[5,7],[3,4],[3,6],[0,5],[5,7],[3,6],[0,1],[0,3],[2,5],[2,6],[1,2],[0,4],[5,7],[0,2],[4,7],[1,7]],[[1,3],[6,7],[3,6],[5,6],[1,5],[3,7],[3,7],[0,6],[3,5],[0,1],[6,7],[1,7],[1,3],[1,5],[0,3],[0,2],[5,7],[0,3],[0,2],[2,7],[2,6],[0,7],[1,2],[0,1],[1,3],[2,7],[0,2],[1,7],[0,7],[2,7],[2,4],[5,7],[1,2],[2,5],[1,5],[0,7],[2,6],[0,3],[3,4],[4,5],[2,5],[0,4],[2,7],[6,7],[2,3],[5,7],[1,7],[1,7],[0,5],[5,6],[1,7],[1,4],[2,7],[1,4],[0,5],[0,6],[4,5],[1,4],[1,4],[5,7],[2,7],[1,3],[1,2],[1,3]],[[3,4],[2,6],[4,5],[0,1],[2,5],[0,5],[0,4],[1,4],[2,6],[3,4],[0,5],[3,5],[4,5],[3,5],[1,6],[5,6],[5,7],[2,3],[1,3],[0,6],[0,1],[0,2],[3,4],[0,6],[3,6],[1,6],[1,4],[4,6],[6,7],[1,4],[0,5],[1,5],[0,5],[4,6],[2,4],[1,4],[6,7],[1,4],[1,7],[1,6],[4,6],[4,7],[1,7],[0,3],[0,7],[3,4],[3,5],[3,7],[1,6],[1,4],[4,7],[2,6],[0,7],[0,6],[3,7],[5,7],[2,3],[1,6],[0,2],[3,6],[6,7],[3,5],[6,7],[3,4]]]
def setup_inputs(rng):
    rt = (0.75 * rng.standard_normal((128, 1), dtype=np.float32) + rng.standard_normal((128, N), dtype=np.float32) / 2).astype(ml_dtypes.bfloat16)
    rm = np.zeros((N, N, TOK), np.float32)
    for r in range(N):
        for t in range(TOK): rm[r, ROUTE[r][t], t] = 1.0
    return {"x": rng.standard_normal((N, 128, TOK), dtype=np.float32).astype(ml_dtypes.bfloat16), "rt": np.broadcast_to(rt, (N, 128, N)).copy(), "rm": rm.astype(ml_dtypes.bfloat16), "w": rng.standard_normal((N, 128, 128), dtype=np.float32).astype(ml_dtypes.bfloat16)}
def setup_inputs_big(rng):
    d = setup_inputs(rng)
    for k in ("x", "w"): d[k] = (d[k].astype(np.float32) * 1024.0).astype(d[k].dtype)
    return d
def setup_inputs_small(rng):
    d = setup_inputs(rng)
    for k in ("x", "w"): d[k] = (d[k].astype(np.float32) * (1 / 1024.0)).astype(d[k].dtype)
    return d
def setup_inputs_apart(rng):
    d = setup_inputs(rng)
    f = (10.0 ** rng.permutation(np.linspace(-1.5, 1.5, N))).astype(np.float32).reshape(N, 1, 1)
    for k in ("x",): d[k] = (d[k].astype(np.float32) * f).astype(d[k].dtype)
    return d
def setup_inputs_lure(rng):
    d = setup_inputs(rng); x = d["x"].astype(np.float32) * 1024; rt = d["rt"][0].astype(np.float32)
    for r in range(N):
        for t in range(TOK):
            u = int(rng.choice([e for e in range(N) if e not in ROUTE[r][t]]))
            x[r][:, t] += 2097152 * (rt[:, u] - rt[:, ROUTE[r][t][0]])
    d["x"] = x.astype(d["x"].dtype)
    return d
def reference(x, rt, rm, w):
    X, RT, W = x.astype(np.float64), rt.astype(np.float64), w.astype(np.float64)
    y = np.zeros((N, 128, TOK))
    for r in range(N):
        sc = RT[r].T @ X[r]
        for t in range(TOK):
            ex = ROUTE[r][t]; g = np.exp(sc[ex, t] - sc[ex, t].max()); g = g / g.sum()
            y[r][:, t] = sum(g[i] * (W[e].T @ X[r][:, t]) for i, e in enumerate(ex))
    return {"y": y.astype(ml_dtypes.bfloat16)}

@@ -1,0 +1,197 @@
+from concourse.mybir import AluOpType, ActivationFunctionType
+
+NX = 8
+TK = 64
+W0, W1 = 0, 128
+X0, X1 = 128, 192
+M0, M1 = 192, 256
+R0, R1 = 256, 264
+
+SCRATCH = {
+    "pack": ("sbuf", [128, 264], "bfloat16"),
+    "ydr": ("dram", [128, 64], "bfloat16"),
+    "pk0": ("sbuf", [128, 264], "bfloat16"),
+    "pk1": ("sbuf", [128, 264], "bfloat16"),
+    "wf": ("sbuf", [128, 768], "bfloat16"),
+    "cm": ("sbuf", [128, 8], "float32"),
+    "sel": ("sbuf", [128, 1024], "bfloat16"),
+    "ms": ("sbuf", [128, 128], "float32"),
+    "sg": ("sbuf", [128, 128], "float32"),
+    "gt": ("sbuf", [128, 128], "bfloat16"),
+    "xg": ("sbuf", [128, 1024], "bfloat16"),
+    "yo": ("sbuf", [128, 128], "bfloat16"),
+    "sd0": ("psum", [128, 512], "float32"), "sd1": ("psum", [128, 512], "float32"),
+    "gl0": ("psum", [128, 512], "float32"), "gl1": ("psum", [128, 512], "float32"),
+    "gh0": ("psum", [128, 512], "float32"), "gh1": ("psum", [128, 512], "float32"),
+    "py0": ("psum", [128, 512], "float32"), "py1": ("psum", [128, 512], "float32"),
+}
+SEMAPHORES = (["fill", "ld", "sent", "yarr", "st", "cst"]
+              + ["a%d" % e for e in range(NX)]
+              + ["%s%d" % (n, j) for n in ("sS", "sM", "sD", "sA", "sG", "sLl", "sLh", "sY", "sC") for j in range(2)]
+              + ["sX%d_%d" % (j, i) for j in range(2) for i in range(NX)])
+
+
+def _plan(T, topo):
+    cores = list(T.cores)
+    pairs, used = [], []
+    for a in cores:
+        if a in used:
+            continue
+        for b in cores:
+            if b != a and b not in used and topo.mates(topo.chip(a), topo.chip(b)):
+                pairs.append((a, b))
+                used += [a, b]
+                break
+    n = topo.CORES_PER_CHIP
+    sites = []
+    for a, b in pairs:
+        best = None
+        for home, far in ((a, b), (b, a)):
+            for c in range(topo.chip(home) * n, (topo.chip(home) + 1) * n):
+                if c in cores or not all(topo.may_write(r, c) for r in cores):
+                    continue
+                if not (topo.may_write(c, a) and topo.may_write(c, b)):
+                    continue
+                score = 0 if topo.die(c) == topo.die(home) else 1
+                if best is None or score < best[0]:
+                    best = (score, c, home, far)
+        sites.append(best[1:])
+    return sites
+
+
+def _bits(m):
+    return bin(m).count("1")
+
+
+def _send(g, topo, src, dst, out, in_, rsem, lsem, mask):
+    rid, pid, _ = topo.addr(dst)
+    g.remote_dma(out, in_, rsem, lsem, pid, rid, mask)
+    return _bits(mask)
+
+
+def _common_mask(topo, src, dsts):
+    m = topo.mask(src, dsts[0])
+    for d in dsts[1:]:
+        m &= topo.mask(src, d)
+    return m
+
+
+def _rank(g, core, T, topo, sites):
+    S = T.sem
+    ns = len(sites)
+    s = [i for i in range(ns) if core in sites[i][1:]][0]
+    home = sites[s][1] == core
+    e = T.rank_of(core)
+    pk = T.pack
+    width = R1 if home else M1
+    g.vector.memset(pk[:, M0:M1], 0.0).then_inc(S.fill, 1)
+    g.sync.dma_start(pk[:, W0:W1], T.w[:, :]).then_inc(S.ld, 16)
+    g.scalar.dma_start(pk[:, X0:X1], T.x[:, :]).then_inc(S.ld, 16)
+    g.scalar.wait_ge(S.fill, 1)
+    g.scalar.dma_start(pk[0:NX, M0:M1], T.rm[:, :]).then_inc(S.ld, 16)
+    nld = 48
+    if home:
+        g.sync.dma_start(pk[:, R0:R1], T.rt[:, :]).then_inc(S.ld, 16)
+        nld += 16
+    g.wait_ge(S.fill, 1)
+    g.wait_ge(S.ld, nld)
+    mask = _common_mask(topo, core, [t[0] for t in sites])
+    arr = S["a%d" % e]
+    land = T.pk0 if home else T.pk1
+    sent = _send(g, topo, core, sites[s][0], land[:, 0:width], pk[:, 0:width], arr, S.sent, mask)
+    for k in range(1, ns):
+        slot = 2 * (k - 1) + (0 if home else 1)
+        sent += _send(g, topo, core, sites[(s + k) % ns][0], T.wf[:, slot * 128:(slot + 1) * 128], pk[:, W0:W1],
+                      arr, S.sent, mask)
+    ny = _bits(_common_mask(topo, sites[s][0], list(sites[s][1:])))
+    g.sync.wait_ge(S.yarr, ny)
+    g.sync.dma_start(T.y[:, :], T.ydr[:, :]).then_inc(S.st, 16)
+    g.sync.wait_ge(S.st, 16)
+    g.wait_ge(S.sent, sent)
+
+
+def _site(g, core, T, topo, sites):
+    S = T.sem
+    ns = len(sites)
+    s = [i for i in range(ns) if sites[i][0] == core][0]
+    pe, dve, act = g.tensor, g.vector, g.scalar
+    mult = AluOpType.mult
+    pks = (T.pk0, T.pk1)
+    sd = (T.sd0, T.sd1)
+    gbank = ((T.gl0, T.gh0), (T.gl1, T.gh1))
+    py = (T.py0, T.py1)
+    order = []
+    for k in range(ns):
+        src = sites[(s - k) % ns]
+        for j in range(2):
+            c = src[1 + j]
+            wap = pks[j][:, W0:W1] if k == 0 else T.wf[:, (2 * (k - 1) + j) * 128:(2 * (k - 1) + j + 1) * 128]
+            order.append((T.rank_of(c), wap, _bits(_common_mask(topo, c, [t[0] for t in sites]))))
+
+    def arrived(q, i):
+        q.wait_ge(S["a%d" % order[i][0]], order[i][2])
+
+    dve.memset(T.cm[0:NX, 0:NX], 1.0).then_inc(S.fill, 1)
+    dve.memset(T.sel[0:NX, :], 1.0).then_inc(S.fill, 1)
+    g.wait_ge(S.fill, 2)
+    g.affine_select(T.cm[0:NX, 0:NX], T.cm[0:NX, 0:NX], [[-1, NX]], AluOpType.is_equal, -1.0, 0, 1).then_inc(S.cst, 1)
+    g.affine_select(T.sel[0:NX, :], T.sel[0:NX, :], [[-1, NX], [0, 128]], AluOpType.is_equal, 0.0, 0, 1).then_inc(S.cst, 1)
+
+    pe.wait_ge(S.cst, 2)
+    for j in range(2):
+        c0, c1 = j * TK, (j + 1) * TK
+        arrived(pe, j)
+        pe.matmul(sd[j][0:NX, 0:TK], T.pk0[:, R0:R1], pks[j][:, X0:X1], True, True).then_inc(S["sS%d" % j], 1)
+        arrived(dve, j)
+        dve.wait_ge(S["sS%d" % j], 1)
+        dve.tensor_tensor(T.ms[0:NX, c0:c1], sd[j][0:NX, 0:TK], pks[j][0:NX, M0:M1], mult).then_inc(S["sM%d" % j], 1)
+        pe.wait_ge(S["sM%d" % j], 1)
+        pe.matmul(sd[j][0:NX, TK:2 * TK], T.cm[0:NX, 0:NX], T.ms[0:NX, c0:c1], True, True).then_inc(S["sD%d" % j], 1)
+        act.wait_ge(S["sD%d" % j], 1)
+        act.activation(T.sg[0:NX, c0:c1], sd[j][0:NX, TK:2 * TK], ActivationFunctionType.Sigmoid).then_inc(S["sA%d" % j], 1)
+    for j in range(2):
+        c0, c1 = j * TK, (j + 1) * TK
+        dve.wait_ge(S["sA%d" % j], 1)
+        dve.tensor_tensor(T.gt[0:NX, c0:c1], T.sg[0:NX, c0:c1], pks[j][0:NX, M0:M1], mult).then_inc(S["sG%d" % j], 1)
+    pe.wait_ge(S.sG0, 1)
+    pe.wait_ge(S.sG1, 1)
+    for h in range(2):
+        for j in (1, 0):
+            for i in range(4 * h, 4 * h + 4):
+                e = order[i][0]
+                pe.matmul(gbank[j][h][:, (i % 4) * TK:(i % 4 + 1) * TK], T.sel[0:NX, e * 128:(e + 1) * 128],
+                          T.gt[0:NX, j * TK:(j + 1) * TK], True, True).then_inc(S["%s%d" % ("sLh" if h else "sLl", j)], 1)
+    for h in range(2):
+        for j in (1, 0):
+            dve.wait_ge(S["%s%d" % ("sLh" if h else "sLl", j)], 4)
+        for i in range(4 * h, 4 * h + 4):
+            for j in (1, 0):
+                dve.tensor_tensor(T.xg[:, (j * NX + i) * TK:(j * NX + i + 1) * TK],
+                                  gbank[j][h][:, (i % 4) * TK:(i % 4 + 1) * TK], pks[j][:, X0:X1], mult
+                                  ).then_inc(S["sX%d_%d" % (j, i)], 1)
+    for i in range(NX):
+        arrived(pe, i)
+        for j in (1, 0):
+            pe.wait_ge(S["sX%d_%d" % (j, i)], 1)
+            mm = pe.matmul(py[j][:, 0:TK], order[i][1], T.xg[:, (j * NX + i) * TK:(j * NX + i + 1) * TK],
+                           i == 0, i == NX - 1)
+            if i == NX - 1:
+                mm.then_inc(S["sY%d" % j], 1)
+    dve.wait_ge(S.sY1, 1)
+    dve.tensor_copy(T.yo[:, TK:2 * TK], py[1][:, 0:TK]).then_inc(S.sC1, 1)
+    act.wait_ge(S.sY0, 1)
+    act.activation(T.yo[:, 0:TK], py[0][:, 0:TK], ActivationFunctionType.Copy).then_inc(S.sC0, 1)
+    mask = _common_mask(topo, core, list(sites[s][1:]))
+    sent = 0
+    for j in (1, 0):
+        g.wait_ge(S["sC%d" % j], 1)
+        sent += _send(g, topo, core, sites[s][1 + j], T.ydr[:, :], T.yo[:, j * TK:(j + 1) * TK], S.yarr, S.sent, mask)
+    g.wait_ge(S.sent, sent)
+
+
+def rank_program(g, core, T, topo):
+    sites = _plan(T, topo)
+    if T.rank_of(core) is not None:
+        _rank(g, core, T, topo, sites)
+    elif core in [t[0] for t in sites]:
+        _site(g, core, T, topo, sites)

@@ -2,196 +2,168 @@ from concourse.mybir import AluOpType, ActivationFunctionType
 
 NX = 8
 TK = 64
-W0, W1 = 0, 128
-X0, X1 = 128, 192
-M0, M1 = 192, 256
-R0, R1 = 256, 264
+ENG = 8
+HOP = 4
 
 SCRATCH = {
-    "pack": ("sbuf", [128, 264], "bfloat16"),
-    "ydr": ("dram", [128, 64], "bfloat16"),
-    "pk0": ("sbuf", [128, 264], "bfloat16"),
-    "pk1": ("sbuf", [128, 264], "bfloat16"),
-    "wf": ("sbuf", [128, 768], "bfloat16"),
+    "wl": ("sbuf", [128, 1024], "bfloat16"),
+    "hw": ("sbuf", [128, 128], "bfloat16"),
+    "xs": ("sbuf", [128, 64], "bfloat16"),
+    "rts": ("sbuf", [128, 8], "bfloat16"),
+    "rms": ("sbuf", [128, 64], "bfloat16"),
+    "i8": ("sbuf", [128, 8], "float32"),
     "cm": ("sbuf", [128, 8], "float32"),
+    "ones": ("sbuf", [128, 128], "bfloat16"),
     "sel": ("sbuf", [128, 1024], "bfloat16"),
-    "ms": ("sbuf", [128, 128], "float32"),
-    "sg": ("sbuf", [128, 128], "float32"),
-    "gt": ("sbuf", [128, 128], "bfloat16"),
-    "xg": ("sbuf", [128, 1024], "bfloat16"),
-    "yo": ("sbuf", [128, 128], "bfloat16"),
-    "sd0": ("psum", [128, 512], "float32"), "sd1": ("psum", [128, 512], "float32"),
-    "gl0": ("psum", [128, 512], "float32"), "gl1": ("psum", [128, 512], "float32"),
-    "gh0": ("psum", [128, 512], "float32"), "gh1": ("psum", [128, 512], "float32"),
-    "py0": ("psum", [128, 512], "float32"), "py1": ("psum", [128, 512], "float32"),
+    "ms": ("sbuf", [128, 64], "float32"),
+    "sg": ("sbuf", [128, 64], "float32"),
+    "gt": ("sbuf", [128, 64], "bfloat16"),
+    "xg": ("sbuf", [128, 512], "bfloat16"),
+    "yo": ("sbuf", [128, 64], "bfloat16"),
+    "sd": ("psum", [128, 512], "float32"),
+    "gl": ("psum", [128, 512], "float32"),
+    "gh": ("psum", [128, 512], "float32"),
+    "py": ("psum", [128, 512], "float32"),
 }
-SEMAPHORES = (["fill", "ld", "sent", "yarr", "st", "cst"]
-              + ["a%d" % e for e in range(NX)]
-              + ["%s%d" % (n, j) for n in ("sS", "sM", "sD", "sA", "sG", "sLl", "sLh", "sY", "sC") for j in range(2)]
-              + ["sX%d_%d" % (j, i) for j in range(2) for i in range(NX)])
+SEMAPHORES = (["fill", "cst", "cs2", "ldw", "ldx", "sent", "harr", "st", "sS", "sM", "sD", "sA", "sG", "sLl", "sLh",
+               "sY", "sC"] + ["a%d" % e for e in range(NX)] + ["sX%d" % i for i in range(NX)])
 
 
 def _plan(T, topo):
     cores = list(T.cores)
-    pairs, used = [], []
-    for a in cores:
-        if a in used:
-            continue
-        for b in cores:
-            if b != a and b not in used and topo.mates(topo.chip(a), topo.chip(b)):
-                pairs.append((a, b))
-                used += [a, b]
-                break
     n = topo.CORES_PER_CHIP
-    sites = []
-    for a, b in pairs:
-        best = None
-        for home, far in ((a, b), (b, a)):
-            for c in range(topo.chip(home) * n, (topo.chip(home) + 1) * n):
-                if c in cores or not all(topo.may_write(r, c) for r in cores):
-                    continue
-                if not (topo.may_write(c, a) and topo.may_write(c, b)):
-                    continue
-                score = 0 if topo.die(c) == topo.die(home) else 1
-                if best is None or score < best[0]:
-                    best = (score, c, home, far)
-        sites.append(best[1:])
-    return sites
+    plan = {}
+    for c in cores:
+        mine = sorted([r for r in cores if r == c or topo.same_plane(topo.chip(c), topo.chip(r))], key=topo.chip)
+        cross = sorted([r for r in cores if r not in mine], key=topo.chip)
+        p = mine.index(c)
+        same_rot = [mine[(p + k) % len(mine)] for k in range(1, len(mine))]
+        cross_rot = [cross[(p + k) % len(cross)] for k in range(len(cross))]
+        base = topo.chip(c) * n
+        hs = [h for h in range(base, base + n) if h not in cores and topo.die(h) == topo.die(c)
+              and all(topo.may_write(h, t) for t in cross)][:2]
+        own_ok = all(topo.may_write(c, t) for t in cross)
+        ncar = len(hs) + (1 if own_ok and len(hs) < 2 else 0)
+        share = -(-len(cross) // ncar)
+        relays = [(h, cross_rot[i * share:(i + 1) * share]) for i, h in enumerate(hs)]
+        plan[c] = (relays, same_rot + cross_rot[len(hs) * share:])
+    return plan
 
 
-def _bits(m):
-    return bin(m).count("1")
+def _arrival_order(T, plan, me):
+    score = {T.rank_of(me): 0}
+    for c, (relays, direct) in plan.items():
+        for i, (h, tg) in enumerate(relays):
+            if me in tg:
+                score[T.rank_of(c)] = i + 1 + HOP + tg.index(me) + 1
+        if me in direct:
+            score[T.rank_of(c)] = len(relays) + direct.index(me) + 1
+    return sorted(score, key=lambda e: (score[e], e))
 
 
-def _send(g, topo, src, dst, out, in_, rsem, lsem, mask):
-    rid, pid, _ = topo.addr(dst)
-    g.remote_dma(out, in_, rsem, lsem, pid, rid, mask)
-    return _bits(mask)
-
-
-def _common_mask(topo, src, dsts):
+def _mask(topo, src, dsts, n):
     m = topo.mask(src, dsts[0])
     for d in dsts[1:]:
         m &= topo.mask(src, d)
-    return m
+    out, k = 0, 0
+    for b in range(16):
+        if (m >> b) & 1 and k < n:
+            out |= 1 << b
+            k += 1
+    return out
 
 
-def _rank(g, core, T, topo, sites):
+def _send(g, topo, dst, out, in_, rsem, lsem, mask):
+    rid, pid, _ = topo.addr(dst)
+    g.remote_dma(out, in_, rsem, lsem, pid, rid, mask)
+
+
+def _helper(g, core, T, topo, e, targets):
     S = T.sem
-    ns = len(sites)
-    s = [i for i in range(ns) if core in sites[i][1:]][0]
-    home = sites[s][1] == core
-    e = T.rank_of(core)
-    pk = T.pack
-    width = R1 if home else M1
-    g.vector.memset(pk[:, M0:M1], 0.0).then_inc(S.fill, 1)
-    g.sync.dma_start(pk[:, W0:W1], T.w[:, :]).then_inc(S.ld, 16)
-    g.scalar.dma_start(pk[:, X0:X1], T.x[:, :]).then_inc(S.ld, 16)
-    g.scalar.wait_ge(S.fill, 1)
-    g.scalar.dma_start(pk[0:NX, M0:M1], T.rm[:, :]).then_inc(S.ld, 16)
-    nld = 48
-    if home:
-        g.sync.dma_start(pk[:, R0:R1], T.rt[:, :]).then_inc(S.ld, 16)
-        nld += 16
-    g.wait_ge(S.fill, 1)
-    g.wait_ge(S.ld, nld)
-    mask = _common_mask(topo, core, [t[0] for t in sites])
-    arr = S["a%d" % e]
-    land = T.pk0 if home else T.pk1
-    sent = _send(g, topo, core, sites[s][0], land[:, 0:width], pk[:, 0:width], arr, S.sent, mask)
-    for k in range(1, ns):
-        slot = 2 * (k - 1) + (0 if home else 1)
-        sent += _send(g, topo, core, sites[(s + k) % ns][0], T.wf[:, slot * 128:(slot + 1) * 128], pk[:, W0:W1],
-                      arr, S.sent, mask)
-    ny = _bits(_common_mask(topo, sites[s][0], list(sites[s][1:])))
-    g.sync.wait_ge(S.yarr, ny)
-    g.sync.dma_start(T.y[:, :], T.ydr[:, :]).then_inc(S.st, 16)
-    g.sync.wait_ge(S.st, 16)
-    g.wait_ge(S.sent, sent)
+    mask = _mask(topo, core, targets, ENG)
+    g.wait_ge(S.harr, ENG)
+    for t in targets:
+        _send(g, topo, t, T.wl[:, e * 128:(e + 1) * 128], T.hw[:, :], S["a%d" % e], S.sent, mask)
+    g.wait_ge(S.sent, ENG * len(targets))
 
 
-def _site(g, core, T, topo, sites):
+def _rank(g, core, T, topo, plan):
     S = T.sem
-    ns = len(sites)
-    s = [i for i in range(ns) if sites[i][0] == core][0]
     pe, dve, act = g.tensor, g.vector, g.scalar
     mult = AluOpType.mult
-    pks = (T.pk0, T.pk1)
-    sd = (T.sd0, T.sd1)
-    gbank = ((T.gl0, T.gh0), (T.gl1, T.gh1))
-    py = (T.py0, T.py1)
-    order = []
-    for k in range(ns):
-        src = sites[(s - k) % ns]
-        for j in range(2):
-            c = src[1 + j]
-            wap = pks[j][:, W0:W1] if k == 0 else T.wf[:, (2 * (k - 1) + j) * 128:(2 * (k - 1) + j + 1) * 128]
-            order.append((T.rank_of(c), wap, _bits(_common_mask(topo, c, [t[0] for t in sites]))))
-
-    def arrived(q, i):
-        q.wait_ge(S["a%d" % order[i][0]], order[i][2])
-
-    dve.memset(T.cm[0:NX, 0:NX], 1.0).then_inc(S.fill, 1)
-    dve.memset(T.sel[0:NX, :], 1.0).then_inc(S.fill, 1)
+    me = T.rank_of(core)
+    relays, direct = plan[core]
+    order = _arrival_order(T, plan, core)
+    own = T.wl[:, me * 128:(me + 1) * 128]
+    g.sync.dma_start(own, T.w[:, :]).then_inc(S.ldw, 16)
+    g.scalar.dma_start(T.xs[:, :], T.x[:, :]).then_inc(S.ldx, 16)
+    g.scalar.dma_start(T.rms[0:NX, :], T.rm[:, :]).then_inc(S.ldx, 16)
+    g.sync.dma_start(T.rts[:, :], T.rt[:, :]).then_inc(S.ldx, 16)
+    i8 = T.i8[0:NX, 0:NX]
+    dve.memset(i8, 1.0).then_inc(S.fill, 1)
+    dve.memset(T.ones[0:NX, :], 1.0).then_inc(S.fill, 1)
     g.wait_ge(S.fill, 2)
-    g.affine_select(T.cm[0:NX, 0:NX], T.cm[0:NX, 0:NX], [[-1, NX]], AluOpType.is_equal, -1.0, 0, 1).then_inc(S.cst, 1)
-    g.affine_select(T.sel[0:NX, :], T.sel[0:NX, :], [[-1, NX], [0, 128]], AluOpType.is_equal, 0.0, 0, 1).then_inc(S.cst, 1)
-
-    pe.wait_ge(S.cst, 2)
-    for j in range(2):
-        c0, c1 = j * TK, (j + 1) * TK
-        arrived(pe, j)
-        pe.matmul(sd[j][0:NX, 0:TK], T.pk0[:, R0:R1], pks[j][:, X0:X1], True, True).then_inc(S["sS%d" % j], 1)
-        arrived(dve, j)
-        dve.wait_ge(S["sS%d" % j], 1)
-        dve.tensor_tensor(T.ms[0:NX, c0:c1], sd[j][0:NX, 0:TK], pks[j][0:NX, M0:M1], mult).then_inc(S["sM%d" % j], 1)
-        pe.wait_ge(S["sM%d" % j], 1)
-        pe.matmul(sd[j][0:NX, TK:2 * TK], T.cm[0:NX, 0:NX], T.ms[0:NX, c0:c1], True, True).then_inc(S["sD%d" % j], 1)
-        act.wait_ge(S["sD%d" % j], 1)
-        act.activation(T.sg[0:NX, c0:c1], sd[j][0:NX, TK:2 * TK], ActivationFunctionType.Sigmoid).then_inc(S["sA%d" % j], 1)
-    for j in range(2):
-        c0, c1 = j * TK, (j + 1) * TK
-        dve.wait_ge(S["sA%d" % j], 1)
-        dve.tensor_tensor(T.gt[0:NX, c0:c1], T.sg[0:NX, c0:c1], pks[j][0:NX, M0:M1], mult).then_inc(S["sG%d" % j], 1)
-    pe.wait_ge(S.sG0, 1)
-    pe.wait_ge(S.sG1, 1)
-    for h in range(2):
-        for j in (1, 0):
-            for i in range(4 * h, 4 * h + 4):
-                e = order[i][0]
-                pe.matmul(gbank[j][h][:, (i % 4) * TK:(i % 4 + 1) * TK], T.sel[0:NX, e * 128:(e + 1) * 128],
-                          T.gt[0:NX, j * TK:(j + 1) * TK], True, True).then_inc(S["%s%d" % ("sLh" if h else "sLl", j)], 1)
-    for h in range(2):
-        for j in (1, 0):
-            dve.wait_ge(S["%s%d" % ("sLh" if h else "sLl", j)], 4)
-        for i in range(4 * h, 4 * h + 4):
-            for j in (1, 0):
-                dve.tensor_tensor(T.xg[:, (j * NX + i) * TK:(j * NX + i + 1) * TK],
-                                  gbank[j][h][:, (i % 4) * TK:(i % 4 + 1) * TK], pks[j][:, X0:X1], mult
-                                  ).then_inc(S["sX%d_%d" % (j, i)], 1)
+    g.affine_select(i8, i8, [[-1, NX]], AluOpType.is_equal, 0.0, 0, 1).then_inc(S.cst, 1)
+    dve.wait_ge(S.fill, 2)
+    dve.wait_ge(S.cst, 1)
+    dve.tensor_scalar(T.cm[0:NX, 0:NX], i8, 2.0, -1.0, mult, AluOpType.add).then_inc(S.cs2, 1)
+    for e in range(NX):
+        dve.tensor_scalar(T.sel[0:NX, e * 128:(e + 1) * 128], T.ones[0:NX, :], T.i8[0:NX, e:e + 1], None, mult
+                          ).then_inc(S.cs2, 1)
+    mask = _mask(topo, core, [h for h, _ in relays] + direct, ENG)
+    g.wait_ge(S.ldw, 16)
+    for h, _ in relays:
+        _send(g, topo, h, T.hw[:, :], own, S.harr, S.sent, mask)
+    for t in direct:
+        _send(g, topo, t, own, own, S["a%d" % me], S.sent, mask)
+    pe.wait_ge(S.cs2, NX + 1)
+    pe.wait_ge(S.ldx, 48)
+    pe.matmul(T.sd[0:NX, 0:TK], T.rts[:, :], T.xs[:, :], True, True).then_inc(S.sS, 1)
+    dve.wait_ge(S.ldx, 48)
+    dve.wait_ge(S.sS, 1)
+    dve.tensor_tensor(T.ms[0:NX, :], T.sd[0:NX, 0:TK], T.rms[0:NX, :], mult).then_inc(S.sM, 1)
+    pe.wait_ge(S.sM, 1)
+    pe.matmul(T.sd[0:NX, TK:2 * TK], T.cm[0:NX, 0:NX], T.ms[0:NX, :], True, True).then_inc(S.sD, 1)
+    act.wait_ge(S.sD, 1)
+    act.activation(T.sg[0:NX, :], T.sd[0:NX, TK:2 * TK], ActivationFunctionType.Sigmoid).then_inc(S.sA, 1)
+    dve.wait_ge(S.sA, 1)
+    dve.tensor_tensor(T.gt[0:NX, :], T.sg[0:NX, :], T.rms[0:NX, :], mult).then_inc(S.sG, 1)
+    pe.wait_ge(S.sG, 1)
+    banks = (T.gl, T.gh)
+    lsem = (S.sLl, S.sLh)
     for i in range(NX):
-        arrived(pe, i)
-        for j in (1, 0):
-            pe.wait_ge(S["sX%d_%d" % (j, i)], 1)
-            mm = pe.matmul(py[j][:, 0:TK], order[i][1], T.xg[:, (j * NX + i) * TK:(j * NX + i + 1) * TK],
-                           i == 0, i == NX - 1)
-            if i == NX - 1:
-                mm.then_inc(S["sY%d" % j], 1)
-    dve.wait_ge(S.sY1, 1)
-    dve.tensor_copy(T.yo[:, TK:2 * TK], py[1][:, 0:TK]).then_inc(S.sC1, 1)
-    act.wait_ge(S.sY0, 1)
-    act.activation(T.yo[:, 0:TK], py[0][:, 0:TK], ActivationFunctionType.Copy).then_inc(S.sC0, 1)
-    mask = _common_mask(topo, core, list(sites[s][1:]))
-    sent = 0
-    for j in (1, 0):
-        g.wait_ge(S["sC%d" % j], 1)
-        sent += _send(g, topo, core, sites[s][1 + j], T.ydr[:, :], T.yo[:, j * TK:(j + 1) * TK], S.yarr, S.sent, mask)
-    g.wait_ge(S.sent, sent)
+        e = order[i]
+        pe.matmul(banks[i // 4][:, (i % 4) * TK:(i % 4 + 1) * TK], T.sel[0:NX, e * 128:(e + 1) * 128], T.gt[0:NX, :],
+                  True, True).then_inc(lsem[i // 4], 1)
+    for i in range(NX):
+        if i % 4 == 0:
+            dve.wait_ge(lsem[i // 4], 4)
+        dve.tensor_tensor(T.xg[:, i * TK:(i + 1) * TK], banks[i // 4][:, (i % 4) * TK:(i % 4 + 1) * TK], T.xs[:, :], mult
+                          ).then_inc(S["sX%d" % i], 1)
+    for i in range(NX):
+        e = order[i]
+        if e == me:
+            pe.wait_ge(S.ldw, 16)
+        else:
+            pe.wait_ge(S["a%d" % e], ENG)
+        pe.wait_ge(S["sX%d" % i], 1)
+        mm = pe.matmul(T.py[:, 0:TK], T.wl[:, e * 128:(e + 1) * 128], T.xg[:, i * TK:(i + 1) * TK], i == 0, i == NX - 1)
+        if i == NX - 1:
+            mm.then_inc(S.sY, 1)
+    dve.wait_ge(S.sY, 1)
+    dve.tensor_copy(T.yo[:, :], T.py[:, 0:TK]).then_inc(S.sC, 1)
+    g.sync.wait_ge(S.sC, 1)
+    g.sync.dma_start(T.y[:, :], T.yo[:, :]).then_inc(S.st, 16)
+    g.sync.wait_ge(S.st, 16)
+    g.wait_ge(S.sent, ENG * (len(relays) + len(direct)))
 
 
 def rank_program(g, core, T, topo):
-    sites = _plan(T, topo)
+    plan = _plan(T, topo)
     if T.rank_of(core) is not None:
-        _rank(g, core, T, topo, sites)
-    elif core in [t[0] for t in sites]:
-        _site(g, core, T, topo, sites)
+        _rank(g, core, T, topo, plan)
+        return
+    for c, (relays, _) in plan.items():
+        for h, targets in relays:
+            if h == core:
+                _helper(g, core, T, topo, T.rank_of(c), targets)

@@ -1,23 +1,23 @@
+from concourse.bass import DstId, RemoteDMATransfer
 from concourse.mybir import AluOpType, ActivationFunctionType
 
 NX = 8
 TK = 64
-ENG = 8
-HOP = 4
 
 SCRATCH = {
     "wl": ("sbuf", [128, 1024], "bfloat16"),
-    "hw": ("sbuf", [128, 128], "bfloat16"),
+    "wd": ("dram", [128, 128], "bfloat16"),
     "xs": ("sbuf", [128, 64], "bfloat16"),
     "rts": ("sbuf", [128, 8], "bfloat16"),
     "rms": ("sbuf", [128, 64], "bfloat16"),
     "i8": ("sbuf", [128, 8], "float32"),
+    "ch": ("sbuf", [128, 4], "float32"),
     "cm": ("sbuf", [128, 8], "float32"),
     "ones": ("sbuf", [128, 128], "bfloat16"),
-    "sel": ("sbuf", [128, 1024], "bfloat16"),
     "ms": ("sbuf", [128, 64], "float32"),
     "sg": ("sbuf", [128, 64], "float32"),
     "gt": ("sbuf", [128, 64], "bfloat16"),
+    "rr": ("sbuf", [128, 512], "bfloat16"),
     "xg": ("sbuf", [128, 512], "bfloat16"),
     "yo": ("sbuf", [128, 64], "bfloat16"),
     "sd": ("psum", [128, 512], "float32"),
@@ -25,8 +25,8 @@ SCRATCH = {
     "gh": ("psum", [128, 512], "float32"),
     "py": ("psum", [128, 512], "float32"),
 }
-SEMAPHORES = (["fill", "cst", "cs2", "ldw", "ldx", "sent", "harr", "st", "sS", "sM", "sD", "sA", "sG", "sLl", "sLh",
-               "sY", "sC"] + ["a%d" % e for e in range(NX)] + ["sX%d" % i for i in range(NX)])
+SEMAPHORES = (["fill", "cst", "cs2", "ldw", "ldo", "ldx", "sent", "harr", "st", "sS", "sM", "sD", "sA", "sG", "sRl",
+               "sRh", "sLl", "sLh", "sY", "sC"] + ["a%d" % e for e in range(NX)] + ["sX%d" % i for i in range(NX)])
 
 
 def _plan(T, topo):
@@ -34,57 +34,57 @@ def _plan(T, topo):
     n = topo.CORES_PER_CHIP
     plan = {}
     for c in cores:
-        mine = sorted([r for r in cores if r == c or topo.same_plane(topo.chip(c), topo.chip(r))], key=topo.chip)
+        ch = topo.chip(c)
+        mine = sorted([r for r in cores if r == c or topo.same_plane(ch, topo.chip(r))], key=topo.chip)
         cross = sorted([r for r in cores if r not in mine], key=topo.chip)
         p = mine.index(c)
         same_rot = [mine[(p + k) % len(mine)] for k in range(1, len(mine))]
         cross_rot = [cross[(p + k) % len(cross)] for k in range(len(cross))]
-        base = topo.chip(c) * n
-        hs = [h for h in range(base, base + n) if h not in cores and topo.die(h) == topo.die(c)
-              and all(topo.may_write(h, t) for t in cross)][:2]
-        own_ok = all(topo.may_write(c, t) for t in cross)
-        ncar = len(hs) + (1 if own_ok and len(hs) < 2 else 0)
-        share = -(-len(cross) // ncar)
-        relays = [(h, cross_rot[i * share:(i + 1) * share]) for i, h in enumerate(hs)]
-        plan[c] = (relays, same_rot + cross_rot[len(hs) * share:])
+        near = [t for t in cross_rot if topo.mates(ch, topo.chip(t))]
+        far = [t for t in cross_rot if t not in near]
+        owners = [h for h in range(ch * n, ch * n + n) if h not in cores and all(topo.may_write(h, t) for t in cross)]
+        hx = [h for h in owners if topo.die(h) == topo.die(c)][0]
+        hy = [h for h in owners if topo.die(h) != topo.die(c)][0]
+        plan[c] = ([(hx, far[0::2]), (hy, near + far[1::2])], same_rot)
     return plan
 
 
 def _arrival_order(T, plan, me):
     score = {T.rank_of(me): 0}
     for c, (relays, direct) in plan.items():
-        for i, (h, tg) in enumerate(relays):
+        for h, tg in relays:
             if me in tg:
-                score[T.rank_of(c)] = i + 1 + HOP + tg.index(me) + 1
+                score[T.rank_of(c)] = 100 + tg.index(me)
         if me in direct:
-            score[T.rank_of(c)] = len(relays) + direct.index(me) + 1
+            score[T.rank_of(c)] = 1 + direct.index(me)
     return sorted(score, key=lambda e: (score[e], e))
 
 
-def _mask(topo, src, dsts, n):
+def _mask(topo, src, dsts):
     m = topo.mask(src, dsts[0])
     for d in dsts[1:]:
         m &= topo.mask(src, d)
-    out, k = 0, 0
-    for b in range(16):
-        if (m >> b) & 1 and k < n:
-            out |= 1 << b
-            k += 1
-    return out
+    return m, sum((m >> b) & 1 for b in range(16))
 
 
-def _send(g, topo, dst, out, in_, rsem, lsem, mask):
-    rid, pid, _ = topo.addr(dst)
-    g.remote_dma(out, in_, rsem, lsem, pid, rid, mask)
+def _fan(g, topo, dsts, out, in_, rsem, lsem, mask):
+    ids = [DstId(rid=topo.addr(d)[0], pnc=topo.addr(d)[1]) for d in dsts]
+    g.remote_dma_fused([RemoteDMATransfer(dst_ids=ids, dma_engine_mask=mask, remote_sem=rsem, srcs=[in_],
+                                          dsts=[out for _ in dsts], alu_op=0)], local_sem=lsem)
 
 
-def _helper(g, core, T, topo, e, targets):
+def _carrier(g, core, T, topo, src, e, j, targets):
     S = T.sem
-    mask = _mask(topo, core, targets, ENG)
-    g.wait_ge(S.harr, ENG)
-    for t in targets:
-        _send(g, topo, t, T.wl[:, e * 128:(e + 1) * 128], T.hw[:, :], S["a%d" % e], S.sent, mask)
-    g.wait_ge(S.sent, ENG * len(targets))
+    half = NX // 2
+    mask, k = _mask(topo, core, targets + [src])
+    g.vector.memset(T.ch[:, :], 1.0).then_inc(S.fill, 1)
+    g.wait_ge(S.fill, 1)
+    g.affine_select(T.ch[:, :], T.ch[:, :], [[-1, half]], AluOpType.is_equal, 0.0, -half * j, 1).then_inc(S.cs2, 1)
+    g.wait_ge(S.cs2, 1)
+    _fan(g, topo, [src], T.i8[:, half * j:half * (j + 1)], T.ch[:, :], S.cst, S.sent, mask)
+    g.wait_ge(S.harr, _mask(topo, src, [core])[1])
+    _fan(g, topo, targets, T.wl[:, e * 128:(e + 1) * 128], T.wd[:, :], S["a%d" % e], S.sent, mask)
+    g.wait_ge(S.sent, 2 * k)
 
 
 def _rank(g, core, T, topo, plan):
@@ -94,46 +94,56 @@ def _rank(g, core, T, topo, plan):
     me = T.rank_of(core)
     relays, direct = plan[core]
     order = _arrival_order(T, plan, core)
+    adds = {}
+    for c, (rl, dr) in plan.items():
+        if core in dr:
+            adds[T.rank_of(c)] = _mask(topo, c, dr)[1]
+        for h, tg in rl:
+            if core in tg:
+                adds[T.rank_of(c)] = _mask(topo, h, tg + [c])[1]
     own = T.wl[:, me * 128:(me + 1) * 128]
-    g.sync.dma_start(own, T.w[:, :]).then_inc(S.ldw, 16)
+    g.sync.dma_start(T.wd[:, :], T.w[:, :]).then_inc(S.ldw, 16)
     g.scalar.dma_start(T.xs[:, :], T.x[:, :]).then_inc(S.ldx, 16)
     g.scalar.dma_start(T.rms[0:NX, :], T.rm[:, :]).then_inc(S.ldx, 16)
     g.sync.dma_start(T.rts[:, :], T.rt[:, :]).then_inc(S.ldx, 16)
-    i8 = T.i8[0:NX, 0:NX]
-    dve.memset(i8, 1.0).then_inc(S.fill, 1)
+    g.scalar.dma_start(own, T.w[:, :]).then_inc(S.ldo, 16)
+    cm = T.cm[0:NX, 0:NX]
+    dve.memset(cm, 1.0).then_inc(S.fill, 1)
     dve.memset(T.ones[0:NX, :], 1.0).then_inc(S.fill, 1)
     g.wait_ge(S.fill, 2)
-    g.affine_select(i8, i8, [[-1, NX]], AluOpType.is_equal, 0.0, 0, 1).then_inc(S.cst, 1)
-    dve.wait_ge(S.fill, 2)
-    dve.wait_ge(S.cst, 1)
-    dve.tensor_scalar(T.cm[0:NX, 0:NX], i8, 2.0, -1.0, mult, AluOpType.add).then_inc(S.cs2, 1)
-    for e in range(NX):
-        dve.tensor_scalar(T.sel[0:NX, e * 128:(e + 1) * 128], T.ones[0:NX, :], T.i8[0:NX, e:e + 1], None, mult
-                          ).then_inc(S.cs2, 1)
-    mask = _mask(topo, core, [h for h, _ in relays] + direct, ENG)
+    g.affine_select(cm, cm, [[-1, NX]], AluOpType.is_equal, -1.0, 0, 1).then_inc(S.cs2, 1)
+    hs = [h for h, _ in relays]
+    mh, kh = _mask(topo, core, hs)
+    md, kd = _mask(topo, core, direct)
     g.wait_ge(S.ldw, 16)
-    for h, _ in relays:
-        _send(g, topo, h, T.hw[:, :], own, S.harr, S.sent, mask)
-    for t in direct:
-        _send(g, topo, t, own, own, S["a%d" % me], S.sent, mask)
-    pe.wait_ge(S.cs2, NX + 1)
+    _fan(g, topo, hs, T.wd[:, :], T.wd[:, :], S.harr, S.sent, mh)
+    _fan(g, topo, direct, own, T.wd[:, :], S["a%d" % me], S.sent, md)
     pe.wait_ge(S.ldx, 48)
     pe.matmul(T.sd[0:NX, 0:TK], T.rts[:, :], T.xs[:, :], True, True).then_inc(S.sS, 1)
     dve.wait_ge(S.ldx, 48)
     dve.wait_ge(S.sS, 1)
     dve.tensor_tensor(T.ms[0:NX, :], T.sd[0:NX, 0:TK], T.rms[0:NX, :], mult).then_inc(S.sM, 1)
+    pe.wait_ge(S.cs2, 1)
     pe.wait_ge(S.sM, 1)
-    pe.matmul(T.sd[0:NX, TK:2 * TK], T.cm[0:NX, 0:NX], T.ms[0:NX, :], True, True).then_inc(S.sD, 1)
+    pe.matmul(T.sd[0:NX, TK:2 * TK], cm, T.ms[0:NX, :], True, True).then_inc(S.sD, 1)
     act.wait_ge(S.sD, 1)
     act.activation(T.sg[0:NX, :], T.sd[0:NX, TK:2 * TK], ActivationFunctionType.Sigmoid).then_inc(S.sA, 1)
     dve.wait_ge(S.sA, 1)
     dve.tensor_tensor(T.gt[0:NX, :], T.sg[0:NX, :], T.rms[0:NX, :], mult).then_inc(S.sG, 1)
-    pe.wait_ge(S.sG, 1)
     banks = (T.gl, T.gh)
+    rsem = (S.sRl, S.sRh)
     lsem = (S.sLl, S.sLh)
+    act.wait_ge(S.cst, sum(_mask(topo, h, tg + [core])[1] for h, tg in relays))
+    act.wait_ge(S.sG, 1)
     for i in range(NX):
         e = order[i]
-        pe.matmul(banks[i // 4][:, (i % 4) * TK:(i % 4 + 1) * TK], T.sel[0:NX, e * 128:(e + 1) * 128], T.gt[0:NX, :],
+        act.activation(T.rr[0:NX, i * TK:(i + 1) * TK], T.gt[0:NX, :], ActivationFunctionType.Copy,
+                       scale=T.i8[0:NX, e:e + 1]).then_inc(rsem[i // 4], 1)
+    pe.wait_ge(S.fill, 2)
+    for i in range(NX):
+        if i % 4 == 0:
+            pe.wait_ge(rsem[i // 4], 4)
+        pe.matmul(banks[i // 4][:, (i % 4) * TK:(i % 4 + 1) * TK], T.ones[0:NX, :], T.rr[0:NX, i * TK:(i + 1) * TK],
                   True, True).then_inc(lsem[i // 4], 1)
     for i in range(NX):
         if i % 4 == 0:
@@ -143,9 +153,9 @@ def _rank(g, core, T, topo, plan):
     for i in range(NX):
         e = order[i]
         if e == me:
-            pe.wait_ge(S.ldw, 16)
+            pe.wait_ge(S.ldo, 16)
         else:
-            pe.wait_ge(S["a%d" % e], ENG)
+            pe.wait_ge(S["a%d" % e], adds[e])
         pe.wait_ge(S["sX%d" % i], 1)
         mm = pe.matmul(T.py[:, 0:TK], T.wl[:, e * 128:(e + 1) * 128], T.xg[:, i * TK:(i + 1) * TK], i == 0, i == NX - 1)
         if i == NX - 1:
@@ -155,7 +165,7 @@ def _rank(g, core, T, topo, plan):
     g.sync.wait_ge(S.sC, 1)
     g.sync.dma_start(T.y[:, :], T.yo[:, :]).then_inc(S.st, 16)
     g.sync.wait_ge(S.st, 16)
-    g.wait_ge(S.sent, ENG * (len(relays) + len(direct)))
+    g.wait_ge(S.sent, kh + kd)
 
 
 def rank_program(g, core, T, topo):
@@ -164,6 +174,6 @@ def rank_program(g, core, T, topo):
         _rank(g, core, T, topo, plan)
         return
     for c, (relays, _) in plan.items():
-        for h, targets in relays:
+        for j, (h, targets) in enumerate(relays):
             if h == core:
-                _helper(g, core, T, topo, T.rank_of(c), targets)
+                _carrier(g, core, T, topo, c, T.rank_of(c), j, targets)

@@ -13,6 +13,7 @@ SCRATCH = {
     "i8": ("sbuf", [128, 8], "float32"),
     "ch": ("sbuf", [128, 4], "float32"),
     "cm": ("sbuf", [128, 8], "float32"),
+    "big": ("sbuf", [128, 128], "bfloat16"),
     "ones": ("sbuf", [128, 128], "bfloat16"),
     "ms": ("sbuf", [128, 64], "float32"),
     "sg": ("sbuf", [128, 64], "float32"),
@@ -25,8 +26,9 @@ SCRATCH = {
     "gh": ("psum", [128, 512], "float32"),
     "py": ("psum", [128, 512], "float32"),
 }
-SEMAPHORES = (["fill", "cst", "cs2", "ldw", "ldo", "ldx", "sent", "harr", "st", "sS", "sM", "sD", "sA", "sG", "sRl",
-               "sRh", "sLl", "sLh", "sY", "sC"] + ["a%d" % e for e in range(NX)] + ["sX%d" % i for i in range(NX)])
+SEMAPHORES = (["fill", "f0", "fS", "cst", "cs0", "cs2", "cs3", "sO", "ldw", "ldo", "ldx", "sent", "harr", "st", "sS",
+               "sM", "sD", "sA", "sG", "sRl", "sRh", "sLl", "sLh", "sY", "sC"]
+              + ["a%d" % e for e in range(NX)] + ["sX%d" % i for i in range(NX)])
 
 
 def _plan(T, topo):
@@ -60,11 +62,24 @@ def _arrival_order(T, plan, me):
     return sorted(score, key=lambda e: (score[e], e))
 
 
+def _pieces(T, plan, c):
+    order = _arrival_order(T, plan, c)
+    npl = 1 + len(plan[c][1])
+    own, oth = sorted(order[:npl]), sorted(order[npl:])
+    h = len(oth) // 2
+    return [(own[0], len(own)), (oth[0], h), (oth[0] + h, len(oth) - h)]
+
+
 def _mask(topo, src, dsts):
     m = topo.mask(src, dsts[0])
     for d in dsts[1:]:
         m &= topo.mask(src, d)
     return m, sum((m >> b) & 1 for b in range(16))
+
+
+def _rmask(topo, plan, c):
+    relays, direct = plan[c]
+    return _mask(topo, c, [h for h, _ in relays] + direct)
 
 
 def _fan(g, topo, dsts, out, in_, rsem, lsem, mask):
@@ -73,16 +88,22 @@ def _fan(g, topo, dsts, out, in_, rsem, lsem, mask):
                                           dsts=[out for _ in dsts], alu_op=0)], local_sem=lsem)
 
 
-def _carrier(g, core, T, topo, src, e, j, targets):
+def _piece_to(g, T, topo, dst, c0, n, rsem, mask):
     S = T.sem
-    half = NX // 2
+    ch = T.ch[:, 0:n]
+    g.vector.memset(ch, 1.0).then_inc(S.f0, 1)
+    g.wait_ge(S.f0, 1)
+    g.affine_select(ch, ch, [[-1, n]], AluOpType.is_equal, 0.0, -c0, 1).then_inc(S.cs0, 1)
+    g.wait_ge(S.cs0, 1)
+    _fan(g, topo, [dst], T.i8[:, c0:c0 + n], ch, rsem, S.sent, mask)
+
+
+def _carrier(g, core, T, topo, plan, src, e, j, targets):
+    S = T.sem
     mask, k = _mask(topo, core, targets + [src])
-    g.vector.memset(T.ch[:, :], 1.0).then_inc(S.fill, 1)
-    g.wait_ge(S.fill, 1)
-    g.affine_select(T.ch[:, :], T.ch[:, :], [[-1, half]], AluOpType.is_equal, 0.0, -half * j, 1).then_inc(S.cs2, 1)
-    g.wait_ge(S.cs2, 1)
-    _fan(g, topo, [src], T.i8[:, half * j:half * (j + 1)], T.ch[:, :], S.cst, S.sent, mask)
-    g.wait_ge(S.harr, _mask(topo, src, [core])[1])
+    c0, n = _pieces(T, plan, src)[j]
+    _piece_to(g, T, topo, src, c0, n, S.cst, mask)
+    g.wait_ge(S.harr, _rmask(topo, plan, src)[1])
     _fan(g, topo, targets, T.wl[:, e * 128:(e + 1) * 128], T.wd[:, :], S["a%d" % e], S.sent, mask)
     g.wait_ge(S.sent, 2 * k)
 
@@ -94,10 +115,12 @@ def _rank(g, core, T, topo, plan):
     me = T.rank_of(core)
     relays, direct = plan[core]
     order = _arrival_order(T, plan, core)
+    npl = 1 + len(direct)
+    gorder = order[:npl] + sorted(order[npl:])
     adds = {}
     for c, (rl, dr) in plan.items():
         if core in dr:
-            adds[T.rank_of(c)] = _mask(topo, c, dr)[1]
+            adds[T.rank_of(c)] = _rmask(topo, plan, c)[1]
         for h, tg in rl:
             if core in tg:
                 adds[T.rank_of(c)] = _mask(topo, h, tg + [c])[1]
@@ -107,17 +130,22 @@ def _rank(g, core, T, topo, plan):
     g.scalar.dma_start(T.rms[0:NX, :], T.rm[:, :]).then_inc(S.ldx, 16)
     g.sync.dma_start(T.rts[:, :], T.rt[:, :]).then_inc(S.ldx, 16)
     g.scalar.dma_start(own, T.w[:, :]).then_inc(S.ldo, 16)
+    mr, kr = _rmask(topo, plan, core)
+    nxt = direct[0]
+    prev = [c for c in plan if plan[c][1][0] == core][0]
+    c0, n = _pieces(T, plan, nxt)[2]
+    _piece_to(g, T, topo, nxt, c0, n, S.cs3, mr)
     cm = T.cm[0:NX, 0:NX]
+    dve.memset(T.big[0:NX, :], 30.0).then_inc(S.fS, 1)
     dve.memset(cm, 1.0).then_inc(S.fill, 1)
-    dve.memset(T.ones[0:NX, :], 1.0).then_inc(S.fill, 1)
-    g.wait_ge(S.fill, 2)
+    act.wait_ge(S.fS, 1)
+    act.activation(T.ones[0:NX, :], T.big[0:NX, :], ActivationFunctionType.Sigmoid).then_inc(S.sO, 1)
+    g.wait_ge(S.fill, 1)
     g.affine_select(cm, cm, [[-1, NX]], AluOpType.is_equal, -1.0, 0, 1).then_inc(S.cs2, 1)
     hs = [h for h, _ in relays]
-    mh, kh = _mask(topo, core, hs)
-    md, kd = _mask(topo, core, direct)
     g.wait_ge(S.ldw, 16)
-    _fan(g, topo, hs, T.wd[:, :], T.wd[:, :], S.harr, S.sent, mh)
-    _fan(g, topo, direct, own, T.wd[:, :], S["a%d" % me], S.sent, md)
+    _fan(g, topo, hs, T.wd[:, :], T.wd[:, :], S.harr, S.sent, mr)
+    _fan(g, topo, direct, own, T.wd[:, :], S["a%d" % me], S.sent, mr)
     pe.wait_ge(S.ldx, 48)
     pe.matmul(T.sd[0:NX, 0:TK], T.rts[:, :], T.xs[:, :], True, True).then_inc(S.sS, 1)
     dve.wait_ge(S.ldx, 48)
@@ -136,10 +164,12 @@ def _rank(g, core, T, topo, plan):
     act.wait_ge(S.cst, sum(_mask(topo, h, tg + [core])[1] for h, tg in relays))
     act.wait_ge(S.sG, 1)
     for i in range(NX):
-        e = order[i]
+        e = gorder[i]
+        if i == npl:
+            act.wait_ge(S.cs3, _rmask(topo, plan, prev)[1])
         act.activation(T.rr[0:NX, i * TK:(i + 1) * TK], T.gt[0:NX, :], ActivationFunctionType.Copy,
                        scale=T.i8[0:NX, e:e + 1]).then_inc(rsem[i // 4], 1)
-    pe.wait_ge(S.fill, 2)
+    pe.wait_ge(S.sO, 1)
     for i in range(NX):
         if i % 4 == 0:
             pe.wait_ge(rsem[i // 4], 4)
@@ -150,22 +180,23 @@ def _rank(g, core, T, topo, plan):
             dve.wait_ge(lsem[i // 4], 4)
         dve.tensor_tensor(T.xg[:, i * TK:(i + 1) * TK], banks[i // 4][:, (i % 4) * TK:(i % 4 + 1) * TK], T.xs[:, :], mult
                           ).then_inc(S["sX%d" % i], 1)
-    for i in range(NX):
-        e = order[i]
+    for a in range(NX):
+        e = order[a]
+        i = gorder.index(e)
         if e == me:
             pe.wait_ge(S.ldo, 16)
         else:
             pe.wait_ge(S["a%d" % e], adds[e])
         pe.wait_ge(S["sX%d" % i], 1)
-        mm = pe.matmul(T.py[:, 0:TK], T.wl[:, e * 128:(e + 1) * 128], T.xg[:, i * TK:(i + 1) * TK], i == 0, i == NX - 1)
-        if i == NX - 1:
+        mm = pe.matmul(T.py[:, 0:TK], T.wl[:, e * 128:(e + 1) * 128], T.xg[:, i * TK:(i + 1) * TK], a == 0, a == NX - 1)
+        if a == NX - 1:
             mm.then_inc(S.sY, 1)
     dve.wait_ge(S.sY, 1)
     dve.tensor_copy(T.yo[:, :], T.py[:, 0:TK]).then_inc(S.sC, 1)
     g.sync.wait_ge(S.sC, 1)
     g.sync.dma_start(T.y[:, :], T.yo[:, :]).then_inc(S.st, 16)
     g.sync.wait_ge(S.st, 16)
-    g.wait_ge(S.sent, kh + kd)
+    g.wait_ge(S.sent, 3 * kr)
 
 
 def rank_program(g, core, T, topo):
@@ -176,4 +207,4 @@ def rank_program(g, core, T, topo):
     for c, (relays, _) in plan.items():
         for j, (h, targets) in enumerate(relays):
             if h == core:
-                _carrier(g, core, T, topo, c, T.rank_of(c), j, targets)
+                _carrier(g, core, T, topo, plan, c, T.rank_of(c), j, targets)

@@ -3,6 +3,7 @@ from concourse.mybir import AluOpType, ActivationFunctionType
 
 NX = 8
 TK = 64
+BIG = 1.0e28
 
 SCRATCH = {
     "wl": ("sbuf", [128, 1024], "bfloat16"),
@@ -11,23 +12,24 @@ SCRATCH = {
     "rts": ("sbuf", [128, 8], "bfloat16"),
     "rms": ("sbuf", [128, 64], "bfloat16"),
     "i8": ("sbuf", [128, 8], "float32"),
-    "ch": ("sbuf", [128, 4], "float32"),
+    "ch": ("sbuf", [128, 8], "float32"),
     "cm": ("sbuf", [128, 8], "float32"),
     "big": ("sbuf", [128, 128], "bfloat16"),
-    "ones": ("sbuf", [128, 128], "bfloat16"),
+    "zb": ("sbuf", [128, 128], "bfloat16"),
+    "eb": ("sbuf", [128, 1024], "bfloat16"),
+    "qr": ("sbuf", [128, 64], "float32"),
     "ms": ("sbuf", [128, 64], "float32"),
-    "sg": ("sbuf", [128, 64], "float32"),
     "gt": ("sbuf", [128, 64], "bfloat16"),
-    "rr": ("sbuf", [128, 512], "bfloat16"),
     "xg": ("sbuf", [128, 512], "bfloat16"),
     "yo": ("sbuf", [128, 64], "bfloat16"),
     "sd": ("psum", [128, 512], "float32"),
+    "dd": ("psum", [128, 512], "float32"),
     "gl": ("psum", [128, 512], "float32"),
     "gh": ("psum", [128, 512], "float32"),
     "py": ("psum", [128, 512], "float32"),
 }
-SEMAPHORES = (["fill", "f0", "fS", "cst", "cs0", "cs2", "cs3", "sO", "ldw", "ldo", "ldx", "sent", "harr", "st", "sS",
-               "sM", "sD", "sA", "sG", "sRl", "sRh", "sLl", "sLh", "sY", "sC"]
+SEMAPHORES = (["fS", "cst", "cs0", "cs2", "cs3", "sO", "sQ", "ldw", "ldo", "ldx", "sent", "harr", "st", "sS",
+               "sM", "sD", "sG", "sEl", "sEh", "sLl", "sLh", "sY", "sC"]
               + ["a%d" % e for e in range(NX)] + ["sX%d" % i for i in range(NX)])
 
 
@@ -88,21 +90,13 @@ def _fan(g, topo, dsts, out, in_, rsem, lsem, mask):
                                           dsts=[out for _ in dsts], alu_op=0)], local_sem=lsem)
 
 
-def _piece_to(g, T, topo, dst, c0, n, rsem, mask):
-    S = T.sem
-    ch = T.ch[:, 0:n]
-    g.vector.memset(ch, 1.0).then_inc(S.f0, 1)
-    g.wait_ge(S.f0, 1)
-    g.affine_select(ch, ch, [[-1, n]], AluOpType.is_equal, 0.0, -c0, 1).then_inc(S.cs0, 1)
-    g.wait_ge(S.cs0, 1)
-    _fan(g, topo, [dst], T.i8[:, c0:c0 + n], ch, rsem, S.sent, mask)
-
-
 def _carrier(g, core, T, topo, plan, src, e, j, targets):
     S = T.sem
     mask, k = _mask(topo, core, targets + [src])
     c0, n = _pieces(T, plan, src)[j]
-    _piece_to(g, T, topo, src, c0, n, S.cst, mask)
+    g.iota(T.ch[:, 0:n], [[-1, n]], -c0, 1, allow_small_or_imprecise_dtypes=True).then_inc(S.cs0, 1)
+    g.wait_ge(S.cs0, 1)
+    _fan(g, topo, [src], T.i8[:, c0:c0 + n], T.ch[:, 0:n], S.cst, S.sent, mask)
     g.wait_ge(S.harr, _rmask(topo, plan, src)[1])
     _fan(g, topo, targets, T.wl[:, e * 128:(e + 1) * 128], T.wd[:, :], S["a%d" % e], S.sent, mask)
     g.wait_ge(S.sent, 2 * k)
@@ -134,46 +128,49 @@ def _rank(g, core, T, topo, plan):
     nxt = direct[0]
     prev = [c for c in plan if plan[c][1][0] == core][0]
     c0, n = _pieces(T, plan, nxt)[2]
-    _piece_to(g, T, topo, nxt, c0, n, S.cs3, mr)
+    g.iota(T.ch[:, :], [[-1, NX]], 0, 1, allow_small_or_imprecise_dtypes=True).then_inc(S.cs0, 1)
+    g.wait_ge(S.cs0, 1)
+    _fan(g, topo, [nxt], T.i8[:, c0:c0 + n], T.ch[:, c0:c0 + n], S.cs3, S.sent, mr)
     cm = T.cm[0:NX, 0:NX]
-    dve.memset(T.big[0:NX, :], 30.0).then_inc(S.fS, 1)
-    dve.memset(cm, 1.0).then_inc(S.fill, 1)
+    dve.memset(T.big[0:NX, :], -200.0).then_inc(S.fS, 1)
+    dve.wait_ge(S.cs0, 1)
+    dve.tensor_scalar(cm, T.ch[0:NX, 0:NX], 0.0, 0.5, AluOpType.is_equal, AluOpType.subtract).then_inc(S.cs2, 1)
     act.wait_ge(S.fS, 1)
-    act.activation(T.ones[0:NX, :], T.big[0:NX, :], ActivationFunctionType.Sigmoid).then_inc(S.sO, 1)
-    g.wait_ge(S.fill, 1)
-    g.affine_select(cm, cm, [[-1, NX]], AluOpType.is_equal, -1.0, 0, 1).then_inc(S.cs2, 1)
+    act.activation(T.zb[0:NX, :], T.big[0:NX, :], ActivationFunctionType.Sigmoid).then_inc(S.sO, 1)
     hs = [h for h, _ in relays]
     g.wait_ge(S.ldw, 16)
     _fan(g, topo, hs, T.wd[:, :], T.wd[:, :], S.harr, S.sent, mr)
     _fan(g, topo, direct, own, T.wd[:, :], S["a%d" % me], S.sent, mr)
+    dps = T.dd[0:NX, 0:TK]
     pe.wait_ge(S.ldx, 48)
     pe.matmul(T.sd[0:NX, 0:TK], T.rts[:, :], T.xs[:, :], True, True).then_inc(S.sS, 1)
     dve.wait_ge(S.ldx, 48)
+    dve.tensor_scalar(T.qr[0:NX, :], T.rms[0:NX, :], BIG, None, mult).then_inc(S.sQ, 1)
     dve.wait_ge(S.sS, 1)
     dve.tensor_tensor(T.ms[0:NX, :], T.sd[0:NX, 0:TK], T.rms[0:NX, :], mult).then_inc(S.sM, 1)
     pe.wait_ge(S.cs2, 1)
+    pe.wait_ge(S.sQ, 1)
+    pe.matmul(dps, cm, T.qr[0:NX, :], True, False)
     pe.wait_ge(S.sM, 1)
-    pe.matmul(T.sd[0:NX, TK:2 * TK], cm, T.ms[0:NX, :], True, True).then_inc(S.sD, 1)
+    pe.matmul(dps, cm, T.ms[0:NX, :], False, True).then_inc(S.sD, 1)
     act.wait_ge(S.sD, 1)
-    act.activation(T.sg[0:NX, :], T.sd[0:NX, TK:2 * TK], ActivationFunctionType.Sigmoid).then_inc(S.sA, 1)
-    dve.wait_ge(S.sA, 1)
-    dve.tensor_tensor(T.gt[0:NX, :], T.sg[0:NX, :], T.rms[0:NX, :], mult).then_inc(S.sG, 1)
-    banks = (T.gl, T.gh)
-    rsem = (S.sRl, S.sRh)
-    lsem = (S.sLl, S.sLh)
-    act.wait_ge(S.cst, sum(_mask(topo, h, tg + [core])[1] for h, tg in relays))
-    act.wait_ge(S.sG, 1)
+    act.activation(T.gt[0:NX, :], dps, ActivationFunctionType.Sigmoid, scale=2.0).then_inc(S.sG, 1)
+    esem = (S.sEl, S.sEh)
+    dve.wait_ge(S.sO, 1)
+    dve.wait_ge(S.cst, sum(_mask(topo, h, tg + [core])[1] for h, tg in relays))
     for i in range(NX):
         e = gorder[i]
         if i == npl:
-            act.wait_ge(S.cs3, _rmask(topo, plan, prev)[1])
-        act.activation(T.rr[0:NX, i * TK:(i + 1) * TK], T.gt[0:NX, :], ActivationFunctionType.Copy,
-                       scale=T.i8[0:NX, e:e + 1]).then_inc(rsem[i // 4], 1)
-    pe.wait_ge(S.sO, 1)
+            dve.wait_ge(S.cs3, _rmask(topo, plan, prev)[1])
+        dve.tensor_scalar(T.eb[0:NX, i * 128:(i + 1) * 128], T.zb[0:NX, :], T.i8[0:NX, e:e + 1], None,
+                          AluOpType.is_equal).then_inc(esem[i // 4], 1)
+    banks = (T.gl, T.gh)
+    lsem = (S.sLl, S.sLh)
+    pe.wait_ge(S.sG, 1)
     for i in range(NX):
         if i % 4 == 0:
-            pe.wait_ge(rsem[i // 4], 4)
-        pe.matmul(banks[i // 4][:, (i % 4) * TK:(i % 4 + 1) * TK], T.ones[0:NX, :], T.rr[0:NX, i * TK:(i + 1) * TK],
+            pe.wait_ge(esem[i // 4], 4)
+        pe.matmul(banks[i // 4][:, (i % 4) * TK:(i % 4 + 1) * TK], T.eb[0:NX, i * 128:(i + 1) * 128], T.gt[0:NX, :],
                   True, True).then_inc(lsem[i // 4], 1)
     for i in range(NX):
         if i % 4 == 0:

from concourse.bass import DstId, RemoteDMATransfer
from concourse.mybir import AluOpType, ActivationFunctionType

NX = 8
TK = 64
BIG = 1.0e28

SCRATCH = {
    "wl": ("sbuf", [128, 1024], "bfloat16"),
    "wd": ("dram", [128, 128], "bfloat16"),
    "xs": ("sbuf", [128, 64], "bfloat16"),
    "rts": ("sbuf", [128, 8], "bfloat16"),
    "rms": ("sbuf", [128, 64], "bfloat16"),
    "i8": ("sbuf", [128, 8], "float32"),
    "ch": ("sbuf", [128, 8], "float32"),
    "cm": ("sbuf", [128, 8], "float32"),
    "big": ("sbuf", [128, 128], "bfloat16"),
    "zb": ("sbuf", [128, 128], "bfloat16"),
    "eb": ("sbuf", [128, 1024], "bfloat16"),
    "qr": ("sbuf", [128, 64], "float32"),
    "ms": ("sbuf", [128, 64], "float32"),
    "gt": ("sbuf", [128, 64], "bfloat16"),
    "xg": ("sbuf", [128, 512], "bfloat16"),
    "yo": ("sbuf", [128, 64], "bfloat16"),
    "sd": ("psum", [128, 512], "float32"),
    "dd": ("psum", [128, 512], "float32"),
    "gl": ("psum", [128, 512], "float32"),
    "gh": ("psum", [128, 512], "float32"),
    "py": ("psum", [128, 512], "float32"),
}
SEMAPHORES = (["fS", "cst", "cs0", "cs2", "cs3", "sO", "sQ", "ldw", "ldo", "ldx", "sent", "harr", "st", "sS",
               "sM", "sD", "sG", "sEl", "sEh", "sLl", "sLh", "sY", "sC"]
              + ["a%d" % e for e in range(NX)] + ["sX%d" % i for i in range(NX)])


def _plan(T, topo):
    cores = list(T.cores)
    n = topo.CORES_PER_CHIP
    plan = {}
    for c in cores:
        ch = topo.chip(c)
        mine = sorted([r for r in cores if r == c or topo.same_plane(ch, topo.chip(r))], key=topo.chip)
        cross = sorted([r for r in cores if r not in mine], key=topo.chip)
        p = mine.index(c)
        same_rot = [mine[(p + k) % len(mine)] for k in range(1, len(mine))]
        cross_rot = [cross[(p + k) % len(cross)] for k in range(len(cross))]
        near = [t for t in cross_rot if topo.mates(ch, topo.chip(t))]
        far = [t for t in cross_rot if t not in near]
        owners = [h for h in range(ch * n, ch * n + n) if h not in cores and all(topo.may_write(h, t) for t in cross)]
        hx = [h for h in owners if topo.die(h) == topo.die(c)][0]
        hy = [h for h in owners if topo.die(h) != topo.die(c)][0]
        plan[c] = ([(hx, far[0::2]), (hy, near + far[1::2])], same_rot)
    return plan


def _arrival_order(T, plan, me):
    score = {T.rank_of(me): 0}
    for c, (relays, direct) in plan.items():
        for h, tg in relays:
            if me in tg:
                score[T.rank_of(c)] = 100 + tg.index(me)
        if me in direct:
            score[T.rank_of(c)] = 1 + direct.index(me)
    return sorted(score, key=lambda e: (score[e], e))


def _pieces(T, plan, c):
    order = _arrival_order(T, plan, c)
    npl = 1 + len(plan[c][1])
    own, oth = sorted(order[:npl]), sorted(order[npl:])
    h = len(oth) // 2
    return [(own[0], len(own)), (oth[0], h), (oth[0] + h, len(oth) - h)]


def _mask(topo, src, dsts):
    m = topo.mask(src, dsts[0])
    for d in dsts[1:]:
        m &= topo.mask(src, d)
    return m, sum((m >> b) & 1 for b in range(16))


def _rmask(topo, plan, c):
    relays, direct = plan[c]
    return _mask(topo, c, [h for h, _ in relays] + direct)


def _fan(g, topo, dsts, out, in_, rsem, lsem, mask):
    ids = [DstId(rid=topo.addr(d)[0], pnc=topo.addr(d)[1]) for d in dsts]
    g.remote_dma_fused([RemoteDMATransfer(dst_ids=ids, dma_engine_mask=mask, remote_sem=rsem, srcs=[in_],
                                          dsts=[out for _ in dsts], alu_op=0)], local_sem=lsem)


def _carrier(g, core, T, topo, plan, src, e, j, targets):
    S = T.sem
    mask, k = _mask(topo, core, targets + [src])
    c0, n = _pieces(T, plan, src)[j]
    g.iota(T.ch[:, 0:n], [[-1, n]], -c0, 1, allow_small_or_imprecise_dtypes=True).then_inc(S.cs0, 1)
    g.wait_ge(S.cs0, 1)
    _fan(g, topo, [src], T.i8[:, c0:c0 + n], T.ch[:, 0:n], S.cst, S.sent, mask)
    g.wait_ge(S.harr, _rmask(topo, plan, src)[1])
    _fan(g, topo, targets, T.wl[:, e * 128:(e + 1) * 128], T.wd[:, :], S["a%d" % e], S.sent, mask)
    g.wait_ge(S.sent, 2 * k)


def _rank(g, core, T, topo, plan):
    S = T.sem
    pe, dve, act = g.tensor, g.vector, g.scalar
    mult = AluOpType.mult
    me = T.rank_of(core)
    relays, direct = plan[core]
    order = _arrival_order(T, plan, core)
    npl = 1 + len(direct)
    gorder = order[:npl] + sorted(order[npl:])
    adds = {}
    for c, (rl, dr) in plan.items():
        if core in dr:
            adds[T.rank_of(c)] = _rmask(topo, plan, c)[1]
        for h, tg in rl:
            if core in tg:
                adds[T.rank_of(c)] = _mask(topo, h, tg + [c])[1]
    own = T.wl[:, me * 128:(me + 1) * 128]
    g.sync.dma_start(T.wd[:, :], T.w[:, :]).then_inc(S.ldw, 16)
    g.scalar.dma_start(T.xs[:, :], T.x[:, :]).then_inc(S.ldx, 16)
    g.scalar.dma_start(T.rms[0:NX, :], T.rm[:, :]).then_inc(S.ldx, 16)
    g.sync.dma_start(T.rts[:, :], T.rt[:, :]).then_inc(S.ldx, 16)
    g.scalar.dma_start(own, T.w[:, :]).then_inc(S.ldo, 16)
    mr, kr = _rmask(topo, plan, core)
    nxt = direct[0]
    prev = [c for c in plan if plan[c][1][0] == core][0]
    c0, n = _pieces(T, plan, nxt)[2]
    g.iota(T.ch[:, :], [[-1, NX]], 0, 1, allow_small_or_imprecise_dtypes=True).then_inc(S.cs0, 1)
    g.wait_ge(S.cs0, 1)
    _fan(g, topo, [nxt], T.i8[:, c0:c0 + n], T.ch[:, c0:c0 + n], S.cs3, S.sent, mr)
    cm = T.cm[0:NX, 0:NX]
    dve.memset(T.big[0:NX, :], -200.0).then_inc(S.fS, 1)
    dve.wait_ge(S.cs0, 1)
    dve.tensor_scalar(cm, T.ch[0:NX, 0:NX], 0.0, 0.5, AluOpType.is_equal, AluOpType.subtract).then_inc(S.cs2, 1)
    act.wait_ge(S.fS, 1)
    act.activation(T.zb[0:NX, :], T.big[0:NX, :], ActivationFunctionType.Sigmoid).then_inc(S.sO, 1)
    hs = [h for h, _ in relays]
    g.wait_ge(S.ldw, 16)
    _fan(g, topo, hs, T.wd[:, :], T.wd[:, :], S.harr, S.sent, mr)
    _fan(g, topo, direct, own, T.wd[:, :], S["a%d" % me], S.sent, mr)
    dps = T.dd[0:NX, 0:TK]
    pe.wait_ge(S.ldx, 48)
    pe.matmul(T.sd[0:NX, 0:TK], T.rts[:, :], T.xs[:, :], True, True).then_inc(S.sS, 1)
    dve.wait_ge(S.ldx, 48)
    dve.tensor_scalar(T.qr[0:NX, :], T.rms[0:NX, :], BIG, None, mult).then_inc(S.sQ, 1)
    dve.wait_ge(S.sS, 1)
    dve.tensor_tensor(T.ms[0:NX, :], T.sd[0:NX, 0:TK], T.rms[0:NX, :], mult).then_inc(S.sM, 1)
    pe.wait_ge(S.cs2, 1)
    pe.wait_ge(S.sQ, 1)
    pe.matmul(dps, cm, T.qr[0:NX, :], True, False)
    pe.wait_ge(S.sM, 1)
    pe.matmul(dps, cm, T.ms[0:NX, :], False, True).then_inc(S.sD, 1)
    act.wait_ge(S.sD, 1)
    act.activation(T.gt[0:NX, :], dps, ActivationFunctionType.Sigmoid, scale=2.0).then_inc(S.sG, 1)
    esem = (S.sEl, S.sEh)
    dve.wait_ge(S.sO, 1)
    dve.wait_ge(S.cst, sum(_mask(topo, h, tg + [core])[1] for h, tg in relays))
    for i in range(NX):
        e = gorder[i]
        if i == npl:
            dve.wait_ge(S.cs3, _rmask(topo, plan, prev)[1])
        dve.tensor_scalar(T.eb[0:NX, i * 128:(i + 1) * 128], T.zb[0:NX, :], T.i8[0:NX, e:e + 1], None,
                          AluOpType.is_equal).then_inc(esem[i // 4], 1)
    banks = (T.gl, T.gh)
    lsem = (S.sLl, S.sLh)
    pe.wait_ge(S.sG, 1)
    for i in range(NX):
        if i % 4 == 0:
            pe.wait_ge(esem[i // 4], 4)
        pe.matmul(banks[i // 4][:, (i % 4) * TK:(i % 4 + 1) * TK], T.eb[0:NX, i * 128:(i + 1) * 128], T.gt[0:NX, :],
                  True, True).then_inc(lsem[i // 4], 1)
    for i in range(NX):
        if i % 4 == 0:
            dve.wait_ge(lsem[i // 4], 4)
        dve.tensor_tensor(T.xg[:, i * TK:(i + 1) * TK], banks[i // 4][:, (i % 4) * TK:(i % 4 + 1) * TK], T.xs[:, :], mult
                          ).then_inc(S["sX%d" % i], 1)
    for a in range(NX):
        e = order[a]
        i = gorder.index(e)
        if e == me:
            pe.wait_ge(S.ldo, 16)
        else:
            pe.wait_ge(S["a%d" % e], adds[e])
        pe.wait_ge(S["sX%d" % i], 1)
        mm = pe.matmul(T.py[:, 0:TK], T.wl[:, e * 128:(e + 1) * 128], T.xg[:, i * TK:(i + 1) * TK], a == 0, a == NX - 1)
        if a == NX - 1:
            mm.then_inc(S.sY, 1)
    dve.wait_ge(S.sY, 1)
    dve.tensor_copy(T.yo[:, :], T.py[:, 0:TK]).then_inc(S.sC, 1)
    g.sync.wait_ge(S.sC, 1)
    g.sync.dma_start(T.y[:, :], T.yo[:, :]).then_inc(S.st, 16)
    g.sync.wait_ge(S.st, 16)
    g.wait_ge(S.sent, 3 * kr)


def rank_program(g, core, T, topo):
    plan = _plan(T, topo)
    if T.rank_of(core) is not None:
        _rank(g, core, T, topo, plan)
        return
    for c, (relays, _) in plan.items():
        for j, (h, targets) in enumerate(relays):
            if h == core:
                _carrier(g, core, T, topo, plan, c, T.rank_of(c), j, targets)
